import numpy as np
CORES = [0,1,2,3]
N = 4
ROOT = 3
def setup_inputs(rng):
    return {"x": rng.standard_normal((N, 128, 1024), dtype=np.float32)}
def reference(x):
    return {"y": np.broadcast_to(x[ROOT], x.shape)}

@@ -1,0 +1,45 @@
+from concourse.bass import DstId, RemoteDMATransfer
+
+ROWS, COLS = 128, 1024
+
+SCRATCH = {
+    "land": ("sbuf", [ROWS, COLS], "float32"),
+}
+SEMAPHORES = ["loaded", "read", "arrived", "stored"]
+
+
+def rank_program(g, core, T, topo):
+    rank = T.rank_of(core)
+    if rank is None:
+        return
+    root = T.cores[T.root]
+
+    if core == root:
+        g.scalar.dma_start(T.y[:], T.x[:]).then_inc(T.sem.stored, 16)
+        g.sync.dma_start(T.land[:], T.x[:]).then_inc(T.sem.loaded, 16)
+        g.wait_ge(T.sem.loaded, 16)
+        others = [c for c in T.cores if c != root]
+        ids = []
+        for c in others:
+            rid, pid, _se = topo.addr(c)
+            ids.append(DstId(rid=rid, pnc=pid))
+        g.remote_dma_fused(
+            [RemoteDMATransfer(
+                dst_ids=ids,
+                dma_engine_mask=0xFFFF,
+                remote_sem=T.sem.arrived,
+                srcs=[T.land[:]],
+                dsts=[T.land[:] for _c in others],
+                alu_op=0,
+            )],
+            local_sem=T.sem.read,
+        )
+        g.wait_ge(T.sem.read, 16)
+        g.wait_ge(T.sem.stored, 16)
+    else:
+        h = COLS // 2
+        g.sync.wait_ge(T.sem.arrived, 16)
+        g.sync.dma_start(T.y[:, 0:h], T.land[:, 0:h]).then_inc(T.sem.stored, 16)
+        g.scalar.wait_ge(T.sem.arrived, 16)
+        g.scalar.dma_start(T.y[:, h:COLS], T.land[:, h:COLS]).then_inc(T.sem.stored, 16)
+        g.wait_ge(T.sem.stored, 32)

@@ -1,11 +1,15 @@
 from concourse.bass import DstId, RemoteDMATransfer
 
 ROWS, COLS = 128, 1024
+PIECES = 3
+BOUNDS = [(j * COLS + PIECES - 1) // PIECES for j in range(PIECES + 1)]
+ALL_ENGINES = 0xFFFF
 
 SCRATCH = {
     "land": ("sbuf", [ROWS, COLS], "float32"),
 }
-SEMAPHORES = ["loaded", "read", "arrived", "stored"]
+SEMAPHORES = (["ld%d" % j for j in range(PIECES)] + ["arr%d" % j for j in range(PIECES)]
+              + ["read", "stored"])
 
 
 def rank_program(g, core, T, topo):
@@ -13,33 +17,46 @@ def rank_program(g, core, T, topo):
     if rank is None:
         return
     root = T.cores[T.root]
+    owners = [c for c in T.cores if c != root]
+    queues = [g.sync, g.scalar]
+
+    def cols(t, j):
+        return t[:, BOUNDS[j]:BOUNDS[j + 1]]
 
     if core == root:
+        for j in range(PIECES):
+            queues[j % 2].dma_start(cols(T.land, j), cols(T.x, j)).then_inc(T.sem["ld%d" % j], 16)
+        for j in range(PIECES):
+            rid, pid, _se = topo.addr(owners[j])
+            g.wait_ge(T.sem["ld%d" % j], 16)
+            g.remote_dma(cols(T.land, j), cols(T.land, j), T.sem["arr%d" % j], T.sem.read,
+                         pid, rid, ALL_ENGINES)
+        g.scalar.wait_ge(T.sem.read, 16 * PIECES)
         g.scalar.dma_start(T.y[:], T.x[:]).then_inc(T.sem.stored, 16)
-        g.sync.dma_start(T.land[:], T.x[:]).then_inc(T.sem.loaded, 16)
-        g.wait_ge(T.sem.loaded, 16)
-        others = [c for c in T.cores if c != root]
+        g.wait_ge(T.sem.read, 16 * PIECES)
+        g.wait_ge(T.sem.stored, 16)
+    else:
+        mine = owners.index(core)
+        peers = [c for c in owners if c != core]
         ids = []
-        for c in others:
+        for c in peers:
             rid, pid, _se = topo.addr(c)
             ids.append(DstId(rid=rid, pnc=pid))
+        g.wait_ge(T.sem["arr%d" % mine], 16)
         g.remote_dma_fused(
             [RemoteDMATransfer(
                 dst_ids=ids,
-                dma_engine_mask=0xFFFF,
-                remote_sem=T.sem.arrived,
-                srcs=[T.land[:]],
-                dsts=[T.land[:] for _c in others],
+                dma_engine_mask=ALL_ENGINES,
+                remote_sem=T.sem["arr%d" % mine],
+                srcs=[cols(T.land, mine)],
+                dsts=[cols(T.land, mine) for _c in peers],
                 alu_op=0,
             )],
             local_sem=T.sem.read,
         )
+        for j in range(PIECES):
+            q = queues[j % 2]
+            q.wait_ge(T.sem["arr%d" % j], 16)
+            q.dma_start(cols(T.y, j), cols(T.land, j)).then_inc(T.sem.stored, 16)
         g.wait_ge(T.sem.read, 16)
-        g.wait_ge(T.sem.stored, 16)
-    else:
-        h = COLS // 2
-        g.sync.wait_ge(T.sem.arrived, 16)
-        g.sync.dma_start(T.y[:, 0:h], T.land[:, 0:h]).then_inc(T.sem.stored, 16)
-        g.scalar.wait_ge(T.sem.arrived, 16)
-        g.scalar.dma_start(T.y[:, h:COLS], T.land[:, h:COLS]).then_inc(T.sem.stored, 16)
-        g.wait_ge(T.sem.stored, 32)
+        g.wait_ge(T.sem.stored, 16 * PIECES)

from concourse.bass import DstId, RemoteDMATransfer

ROWS, COLS = 128, 1024
PIECES = 3
BOUNDS = [(j * COLS + PIECES - 1) // PIECES for j in range(PIECES + 1)]
ALL_ENGINES = 0xFFFF

SCRATCH = {
    "land": ("sbuf", [ROWS, COLS], "float32"),
}
SEMAPHORES = (["ld%d" % j for j in range(PIECES)] + ["arr%d" % j for j in range(PIECES)]
              + ["read", "stored"])


def rank_program(g, core, T, topo):
    rank = T.rank_of(core)
    if rank is None:
        return
    root = T.cores[T.root]
    owners = [c for c in T.cores if c != root]
    queues = [g.sync, g.scalar]

    def cols(t, j):
        return t[:, BOUNDS[j]:BOUNDS[j + 1]]

    if core == root:
        for j in range(PIECES):
            queues[j % 2].dma_start(cols(T.land, j), cols(T.x, j)).then_inc(T.sem["ld%d" % j], 16)
        for j in range(PIECES):
            rid, pid, _se = topo.addr(owners[j])
            g.wait_ge(T.sem["ld%d" % j], 16)
            g.remote_dma(cols(T.land, j), cols(T.land, j), T.sem["arr%d" % j], T.sem.read,
                         pid, rid, ALL_ENGINES)
        g.scalar.wait_ge(T.sem.read, 16 * PIECES)
        g.scalar.dma_start(T.y[:], T.x[:]).then_inc(T.sem.stored, 16)
        g.wait_ge(T.sem.read, 16 * PIECES)
        g.wait_ge(T.sem.stored, 16)
    else:
        mine = owners.index(core)
        peers = [c for c in owners if c != core]
        ids = []
        for c in peers:
            rid, pid, _se = topo.addr(c)
            ids.append(DstId(rid=rid, pnc=pid))
        g.wait_ge(T.sem["arr%d" % mine], 16)
        g.remote_dma_fused(
            [RemoteDMATransfer(
                dst_ids=ids,
                dma_engine_mask=ALL_ENGINES,
                remote_sem=T.sem["arr%d" % mine],
                srcs=[cols(T.land, mine)],
                dsts=[cols(T.land, mine) for _c in peers],
                alu_op=0,
            )],
            local_sem=T.sem.read,
        )
        for j in range(PIECES):
            q = queues[j % 2]
            q.wait_ge(T.sem["arr%d" % j], 16)
            q.dma_start(cols(T.y, j), cols(T.land, j)).then_inc(T.sem.stored, 16)
        g.wait_ge(T.sem.read, 16)
        g.wait_ge(T.sem.stored, 16 * PIECES)
